import numpy as np
import ml_dtypes


def mxq(x, axis, fmt="e4m3"):
    dtype, down = {"e4m3": (ml_dtypes.float8_e4m3fn, 7), "e5m2": (ml_dtypes.float8_e5m2, 14)}[fmt]
    v = np.moveaxis(np.asarray(x, np.float32).astype(ml_dtypes.bfloat16).astype(np.float64), axis, -1)
    blocks = v.reshape(v.shape[:-1] + (-1, 32))
    amax = np.abs(blocks).max(-1, keepdims=True)
    byte = np.maximum(np.where(amax > 0, np.frexp(amax)[1] - 1 + 127, 0) - down, 1)
    scale = np.exp2(byte - 127.0)
    codes = (blocks / scale).astype(np.float32).astype(dtype).astype(np.float64)
    return np.moveaxis((codes * scale).reshape(v.shape), -1, axis)


WIDE = False


def mx_kscale(k):
    if not WIDE:
        return np.ones(k)
    levels = np.array([30, -30])
    if k % 512:
        return np.exp2(np.random.permutation(np.resize(levels, k // 32))).repeat(32)
    a = np.empty((k // 512, 16))
    for p in range(k // 512):
        a[p, :8] = np.random.permutation(np.resize(levels, 8))
        for g in range(8):
            far = levels[np.abs(levels - a[p, g]) >= 10]
            a[p, g + 8] = far[np.random.randint(len(far))]
    return np.exp2(a.ravel()).repeat(32)


def f64(x):
    return np.asarray(x).astype(np.float64)


def striped(idx):
    return np.tile(np.asarray(idx).reshape(-1, 16).T, (8, 1)).astype(np.uint16)


def unstriped(offs):
    return offs[:16].T.reshape(-1).astype(np.int64)


def striped8(idx):
    return np.asarray(idx).reshape(8, -1, 16).transpose(0, 2, 1).reshape(128, -1).astype(np.uint16)


def unstriped8(offs):
    return offs.reshape(8, 16, -1).transpose(0, 2, 1).reshape(8, -1).astype(np.int64)


def pick8(x, idx, run):
    r = np.arange(len(x))
    return x[r[:, None], idx[r % (8 * run) // run]]


E2M1 = np.array([0.0, 0.5, 1.0, 1.5, 2.0, 3.0, 4.0, 6.0, -0.0, -0.5, -1.0, -1.5, -2.0, -3.0, -4.0, -6.0])


def pack_weight(w, fmt):
    k, n = w.shape
    w = f64(np.asarray(w, np.float32).astype(ml_dtypes.bfloat16)).reshape(k // 32, 32, n)
    amax = np.abs(w).max(1)
    if fmt in ("e4m3", "e5m2"):
        byte = np.frexp(amax)[1] - 1 + 127 - (7 if fmt == "e4m3" else 14)
    else:
        mant, ex = np.frexp(amax / 6.0)
        byte = np.where(mant > 0.5, ex, ex - 1) + 127
    byte = np.clip(np.where(amax > 0, byte, 1), 1, 254)
    scaled = (w * np.exp2(127.0 - byte)[:, None, :]).reshape(k, n).astype(np.float32)
    by_word = np.ascontiguousarray(scaled.reshape(k // 512, 128, 4, n).transpose(0, 1, 3, 2))
    if fmt in ("e4m3", "e5m2"):
        words = by_word.astype(ml_dtypes.float8_e4m3fn if fmt == "e4m3" else ml_dtypes.float8_e5m2).view(np.uint8)
    else:
        c = by_word.astype(ml_dtypes.float4_e2m1fn).view(np.uint8) & 0xF
        words = (c[..., 0::2] | (c[..., 1::2] << 4)).reshape(k // 512, 128, 2 * n)
    return np.ascontiguousarray(words), np.ascontiguousarray(byte.astype(np.uint8).reshape(k // 512, 16, n))


def unpack_weight(words, scales, fmt):
    g, _, n = scales.shape
    words = np.ascontiguousarray(words).reshape(g, 128, n, -1)
    if fmt in ("e4m3", "e5m2"):
        vals = words.view(ml_dtypes.float8_e4m3fn if fmt == "e4m3" else ml_dtypes.float8_e5m2).astype(np.float64)
    else:
        nib = np.empty((g, 128, n, 4), np.uint8)
        nib[..., 0::2] = words & 0xF
        nib[..., 1::2] = words >> 4
        vals = E2M1[nib]
    vals = vals * np.repeat(np.exp2(scales.astype(np.float64) - 127.0), 8, axis=1)[..., None]
    return vals.transpose(0, 1, 3, 2).reshape(g * 512, n)


K, T, J, R, F, Z, C, N, U = 512, 1024, 256, 512, 512, 1024, 512, 256, 256


def setup_inputs():
    n = np.random.standard_normal
    idx = np.random.permutation(T)[:J]
    idx2 = np.random.permutation(Z)[:J]
    idx3 = np.stack([np.random.permutation(C)[:J] for _ in range(8)])
    idx4 = np.stack([np.random.permutation(C)[:J] for _ in range(8)])
    idx5 = np.random.permutation(C)[:U]
    idx6 = np.random.permutation(C)[:U]
    fk = mx_kscale(K)
    ff = mx_kscale(F)
    fr = mx_kscale(R)
    xtp = pack_weight(n((K, T)) / fk[:, None], "e5m2")
    xop = pack_weight(n((F, Z)) / ff[:, None], "e4m3")
    wp = pack_weight(n((K, R)) * 1 / np.sqrt(K) * fk[:, None] * fr, "e2m1")
    w2p = pack_weight(n((F, R)) * 1 / np.sqrt(F) * ff[:, None] * fr, "e2m1")
    wbp = pack_weight(n((R, N)) * 1 / np.sqrt(R) / fr[:, None], "e2m1")
    wcp = pack_weight(n((R, N)) * 1 / np.sqrt(R) / fr[:, None], "e4m3")
    return {
        "xt_words": xtp[0],
        "xt_scales": xtp[1],
        "xo_words": xop[0],
        "xo_scales": xop[1],
        "w_words": wp[0],
        "w_scales": wp[1],
        "w2_words": w2p[0],
        "w2_scales": w2p[1],
        "wb_words": wbp[0],
        "wb_scales": wbp[1],
        "wc_words": wcp[0],
        "wc_scales": wcp[1],
        "so": (np.random.uniform(0.5, 1.6, (N, 1))).astype(np.float32),
        "offs": striped(idx),
        "offs2": striped(idx2),
        "offs3": striped8(idx3),
        "offs4": striped8(idx4),
        "offs5": striped(idx5),
        "offs6": striped(idx6),
    }


def reference(xt_words, xt_scales, xo_words, xo_scales, w_words, w_scales, w2_words, w2_scales, wb_words, wb_scales, wc_words, wc_scales, so, offs, offs2, offs3, offs4, offs5, offs6):
    idx = unstriped(offs)
    idx2 = unstriped(offs2)
    idx3 = unstriped8(offs3)
    idx4 = unstriped8(offs4)
    idx5 = unstriped(offs5)
    idx6 = unstriped(offs6)
    xtu = unpack_weight(xt_words, xt_scales, "e5m2")
    xou = unpack_weight(xo_words, xo_scales, "e4m3")
    wu = unpack_weight(w_words, w_scales, "e2m1")
    w2u = unpack_weight(w2_words, w2_scales, "e2m1")
    wbu = unpack_weight(wb_words, wb_scales, "e2m1")
    wcu = unpack_weight(wc_words, wc_scales, "e4m3")
    xtidxg = xtu[:, idx]
    a = wu.T @ xtidxg
    xoidx2g = xou[:, idx2]
    b = w2u.T @ xoidx2g
    pa = np.zeros((R, C))
    pa[np.arange(R)[:, None], idx3[np.arange(R) % 512 // 64]] = a
    pb = np.zeros((R, C))
    pb[np.arange(R)[:, None], idx4[np.arange(R) % 512 // 64]] = b
    paq = mxq(pa, 0, "e4m3")
    pbq = mxq(pb, 0, "e4m3")
    p = wbu.T @ paq + wcu.T @ pbq
    y = np.maximum(p[:, idx5] * f64(so), p[:, idx6])
    return y

@@ -1,0 +1,222 @@
+from contextlib import ExitStack
+
+import concourse.mybir as mybir
+
+K, T, J, R, C, N, U = 512, 1024, 256, 512, 512, 256, 256
+FLOPS = 2 * (2 * K * R * J + 2 * R * N * C)
+
+F32 = mybir.dt.float32
+BF16 = mybir.dt.bfloat16
+I32 = mybir.dt.int32
+U32 = mybir.dt.uint32
+U16 = mybir.dt.uint16
+U8 = mybir.dt.uint8
+E4M3X4 = mybir.dt.float8_e4m3fn_x4
+E5M2X4 = mybir.dt.float8_e5m2_x4
+E2M1X4 = mybir.dt.float4_e2m1fn_x4
+COPY = mybir.ActivationFunctionType.Copy
+MAX = mybir.AluOpType.max
+
+P = 128
+PACK = 4
+HALF = J // 2
+CH = C // 2
+
+
+def tile_list_boardssum_kernel(tc, xt_words, xt_scales, xo_words, xo_scales, w_words, w_scales,
+                                     w2_words, w2_scales, wb_words, wb_scales, wc_words, wc_scales,
+                                     so, offs, offs2, offs3, offs4, offs5, offs6, out):
+    nc = tc.nc
+    with ExitStack() as ctx:
+        lists = ctx.enter_context(tc.tile_pool(name="lists", bufs=1))
+        keep = ctx.enter_context(tc.tile_pool(name="keep", bufs=1))
+        ring = ctx.enter_context(tc.tile_pool(name="ring", bufs=6))
+        psum = ctx.enter_context(tc.psum_pool(name="psum", bufs=1))
+
+        def sb(name, width, dtype):
+            return keep.tile([P, width], dtype, name=name, align_bytes=64)
+
+        def load_list(name, src):
+            tile = lists.tile([P, J // 16], U16, name=name)
+            nc.sync.dma_start(tile[:], src)
+            return tile
+
+        def load_words(name, src, width, dtype):
+            tile = sb(name, width, dtype)
+            nc.sync.dma_start(tile[:].bitcast(I32), src.bitcast(I32))
+            return tile
+
+        def zero_plane(name, width):
+            tile = sb(name, width, U8)
+            nc.vector.memset(tile[:].bitcast(I32), 0)
+            return tile
+
+        def stage_scales(name, src, width):
+            tile = keep.tile([P, 2, width // 4], I32, name=name)
+            rows = src[0].bitcast(I32).rearrange("(h q r) n -> h r q n", h=2, q=2)
+            for h in range(2):
+                nc.sync.dma_start(tile[64 * h:64 * h + 4, :, :], rows[h])
+            return tile
+
+        def spread_scales(plane, stage):
+            for q in range(4):
+                first = 64 * (q // 2)
+                nc.vector.tensor_copy(plane[32 * q:32 * q + 4, :].bitcast(I32), stage[first:first + 4, q % 2, :])
+
+        def load_plane(plane, src):
+            rows = src[0].bitcast(I32)
+            for q in range(4):
+                nc.sync.dma_start(plane[32 * q:32 * q + 4, :].bitcast(I32), rows[4 * q:4 * q + 4, :])
+
+        def deal(dst, src):
+            nc.vector.tensor_copy(dst.rearrange("p (t m) -> p t m", t=PACK), src.rearrange("p (m t) -> p t m", t=PACK))
+
+        def fp8_words(ap):
+            return ap[0].rearrange("p n t -> p (n t)")
+
+        o1 = load_list("o1", offs)
+        xt_stage = stage_scales("xt_stage", xt_scales, T)
+        w_stage = stage_scales("w_stage", w_scales, R)
+        xt_w = load_words("xt_w", fp8_words(xt_words), T, U32)
+        w_w = load_words("w_w", w_words[0], 2 * R, U8)
+        o3 = load_list("o3", offs3)
+
+        xt_s = zero_plane("xt_s", T)
+        w_s = zero_plane("w_s", R)
+        xo_s = zero_plane("xo_s", T)
+        rest_s = zero_plane("rest_s", R + 2 * N)
+        w2_s, wb_s, wc_s = rest_s[:, 0:R], rest_s[:, R:R + N], rest_s[:, R + N:R + 2 * N]
+
+        o2 = load_list("o2", offs2)
+        load_plane(xo_s, xo_scales)
+        load_plane(w2_s, w2_scales)
+        xo_w = load_words("xo_w", fp8_words(xo_words), T, U32)
+        w2_w = load_words("w2_w", w2_words[0], 2 * R, U8)
+        o4 = load_list("o4", offs4)
+        load_plane(wb_s, wb_scales)
+        load_plane(wc_s, wc_scales)
+        wb_w = load_words("wb_w", wb_words[0], 2 * N, U8)
+        wc_w = load_words("wc_w", fp8_words(wc_words), N, U32)
+        o5 = load_list("o5", offs5)
+        o6 = load_list("o6", offs6)
+        so_t = []
+        for i in range(2):
+            s = keep.tile([P, 1], F32, name="so%d" % i)
+            nc.sync.dma_start(s[:], so[P * i:P * (i + 1), :])
+            so_t.append(s)
+
+        def new_board():
+            board = ring.tile([P, C], F32, name="board", tag="board")
+            nc.vector.memset(board[:], 0.0)
+            return board
+
+        def bank(tag, name):
+            return psum.tile([P, 512], F32, name=name, tag=tag)
+
+        def first_stage(dst, wd, sd, t, xg, sg, fmt, j0, j1):
+            nc.tensor.matmul_mx(out=dst, lhsT=wd[:, 2 * P * t:2 * P * (t + 1)].bitcast(E2M1X4),
+                                lhsT_scale=sd[:, P * t:P * (t + 1)], rhs=xg[:, j0:j1].bitcast(fmt),
+                                rhs_scale=sg[:, j0:j1], start=True, stop=True)
+
+        def scatter(board, o, src, j0, j1):
+            nc.scalar.activation(board[:].indirect(o[:, j0 // 16:j1 // 16]), src, COPY)
+
+        def weave(x4, board, t):
+            nc.vector.tensor_copy(x4[:, t:PACK * C:PACK], board[:])
+
+        boards_a = [new_board() for t in range(PACK)]
+        spread_scales(xt_s, xt_stage)
+        spread_scales(w_s, w_stage)
+        xt_g = sb("xt_g", J, U32)
+        xt_gs = sb("xt_gs", J, U8)
+        w_d = sb("w_d", 2 * R, U8)
+        w_ds = sb("w_ds", R, U8)
+        nc.vector.tensor_copy(xt_gs[:, 0:HALF], xt_s[:].indirect(o1[:, 0:HALF // 16]))
+        deal(w_ds[:], w_s[:])
+        deal(w_d[:].bitcast(U16), w_w[:].bitcast(U16))
+        nc.vector.tensor_copy(xt_g[:, 0:HALF], xt_w[:].indirect(o1[:, 0:HALF // 16]))
+        nc.vector.tensor_copy(xt_gs[:, HALF:J], xt_s[:].indirect(o1[:, HALF // 16:J // 16]))
+        nc.vector.tensor_copy(xt_g[:, HALF:J], xt_w[:].indirect(o1[:, HALF // 16:J // 16]))
+
+        a_sb = sb("a_sb", PACK * J, F32)
+        s0 = bank("s0", "a0")
+        first_stage(s0[:, 0:HALF], w_d, w_ds, 0, xt_g, xt_gs, E5M2X4, 0, HALF)
+        nc.scalar.activation(a_sb[:, 0:HALF], s0[:, 0:HALF], COPY)
+        scatter(boards_a[0], o3, a_sb[:, 0:HALF], 0, HALF)
+        s1 = bank("s1", "a1")
+        first_stage(s1[:, 0:HALF], w_d, w_ds, 0, xt_g, xt_gs, E5M2X4, HALF, J)
+        first_stage(s1[:, HALF:HALF + J], w_d, w_ds, 1, xt_g, xt_gs, E5M2X4, 0, J)
+        nc.vector.tensor_copy(a_sb[:, HALF:2 * J], s1[:, 0:HALF + J])
+        s2 = bank("s2", "a2")
+        for t in (2, 3):
+            first_stage(s2[:, (t - 2) * J:(t - 1) * J], w_d, w_ds, t, xt_g, xt_gs, E5M2X4, 0, J)
+        nc.vector.tensor_copy(a_sb[:, 2 * J:4 * J], s2[:])
+        scatter(boards_a[0], o3, a_sb[:, HALF:J], HALF, J)
+        for t in range(1, PACK):
+            scatter(boards_a[t], o3, a_sb[:, t * J:(t + 1) * J], 0, J)
+
+        xo_g = sb("xo_g", J, U32)
+        xo_gs = sb("xo_gs", J, U8)
+        w2_d = sb("w2_d", 2 * R, U8)
+        w2_ds = sb("w2_ds", R, U8)
+        nc.vector.tensor_copy(xo_gs[:], xo_s[:].indirect(o2[:]))
+        nc.vector.tensor_copy(xo_g[:], xo_w[:].indirect(o2[:]))
+        deal(w2_ds[:], w2_s)
+        deal(w2_d[:].bitcast(U16), w2_w[:].bitcast(U16))
+        b_sb = sb("b_sb", PACK * J, F32)
+        for pair, tag in enumerate(("s3", "s0")):
+            sbank = bank(tag, "b%d" % pair)
+            for e in range(2):
+                first_stage(sbank[:, e * J:(e + 1) * J], w2_d, w2_ds, 2 * pair + e, xo_g, xo_gs, E4M3X4, 0, J)
+            nc.vector.tensor_copy(b_sb[:, 2 * pair * J:2 * (pair + 1) * J], sbank[:])
+
+        pa4 = sb("pa4", PACK * C, BF16)
+        for t in range(PACK):
+            weave(pa4, boards_a[t], t)
+        qa = sb("qa", C, U32)
+        qa_s = sb("qa_s", C, U8)
+        nc.vector.quantize_mx(out=qa[:].bitcast(E4M3X4), scales=qa_s[:], in_=pa4[:])
+        acc = [[bank("p%d%d" % (i, h), "p%d%d" % (i, h)) for h in range(2)] for i in range(2)]
+        for i in range(2):
+            for h in range(2):
+                nc.tensor.matmul_mx(out=acc[i][h][:, 0:CH], lhsT=wb_w[:, 2 * P * i:2 * P * (i + 1)].bitcast(E2M1X4),
+                                    lhsT_scale=wb_s[:, P * i:P * (i + 1)], rhs=qa[:, CH * h:CH * (h + 1)].bitcast(E4M3X4),
+                                    rhs_scale=qa_s[:, CH * h:CH * (h + 1)], start=True, stop=False)
+
+        pb4 = sb("pb4", PACK * C, BF16)
+        qb = sb("qb", C, U32)
+        qb_s = sb("qb_s", C, U8)
+        for t in range(PACK):
+            board = new_board()
+            scatter(board, o4, b_sb[:, t * J:(t + 1) * J], 0, J)
+            if t < PACK - 1:
+                weave(pb4, board, t)
+        last = PACK - 1
+        for h in range(2):
+            nc.vector.tensor_copy(pb4[:, PACK * CH * h + last:PACK * CH * (h + 1):PACK], board[:, CH * h:CH * (h + 1)])
+        p_sb = [sb("p_sb%d" % i, C, F32) for i in range(2)]
+        for h in range(2):
+            cols = slice(CH * h, CH * (h + 1))
+            nc.vector.quantize_mx(out=qb[:, cols].bitcast(E4M3X4), scales=qb_s[:, cols],
+                                  in_=pb4[:, PACK * CH * h:PACK * CH * (h + 1)])
+            for i in range(2):
+                nc.tensor.matmul_mx(out=acc[i][h][:, 0:CH], lhsT=wc_w[:, P * i:P * (i + 1)].bitcast(E4M3X4),
+                                    lhsT_scale=wc_s[:, P * i:P * (i + 1)], rhs=qb[:, cols].bitcast(E4M3X4),
+                                    rhs_scale=qb_s[:, cols], start=False, stop=True)
+        for h in range(2):
+            cols = slice(CH * h, CH * (h + 1))
+            nc.scalar.activation(p_sb[0][:, cols], acc[0][h][:, 0:CH], COPY)
+            nc.vector.tensor_copy(p_sb[1][:, cols], acc[1][h][:, 0:CH])
+
+        picked, scaled = [], []
+        for i in range(2):
+            sc = sb("scaled%d" % i, U, F32)
+            nc.scalar.activation(sc[:], p_sb[i][:].indirect(o5[:]), COPY, scale=so_t[i][:])
+            pk = sb("picked%d" % i, U, F32)
+            nc.vector.tensor_copy(pk[:], p_sb[i][:].indirect(o6[:]))
+            scaled.append(sc)
+            picked.append(pk)
+        for i in range(2):
+            y = sb("y%d" % i, U, F32)
+            nc.vector.tensor_tensor(y[:], scaled[i][:], picked[i][:], MAX)
+            nc.sync.dma_start(out[P * i:P * (i + 1), :], y[:])

@@ -30,20 +30,20 @@ def tile_list_boardssum_kernel(tc, xt_words, xt_scales, xo_words, xo_scales, w_w
     with ExitStack() as ctx:
         lists = ctx.enter_context(tc.tile_pool(name="lists", bufs=1))
         keep = ctx.enter_context(tc.tile_pool(name="keep", bufs=1))
-        ring = ctx.enter_context(tc.tile_pool(name="ring", bufs=6))
+        ring = ctx.enter_context(tc.tile_pool(name="ring", bufs=8))
         psum = ctx.enter_context(tc.psum_pool(name="psum", bufs=1))
 
-        def sb(name, width, dtype):
-            return keep.tile([P, width], dtype, name=name, align_bytes=64)
+        def sb(name, width, dtype, tag=""):
+            return keep.tile([P, width], dtype, name=name, tag=tag, align_bytes=64)
 
         def load_list(name, src):
             tile = lists.tile([P, J // 16], U16, name=name)
             nc.sync.dma_start(tile[:], src)
             return tile
 
-        def load_words(name, src, width, dtype):
-            tile = sb(name, width, dtype)
-            nc.sync.dma_start(tile[:].bitcast(I32), src.bitcast(I32))
+        def load_words(name, src, width, dtype, tag="", queue=nc.sync):
+            tile = keep.tile([P, width], dtype, name=name, tag=tag, align_bytes=64)
+            queue.dma_start(tile[:].bitcast(I32), src.bitcast(I32))
             return tile
 
         def zero_plane(name, width):
@@ -51,11 +51,11 @@ def tile_list_boardssum_kernel(tc, xt_words, xt_scales, xo_words, xo_scales, w_w
             nc.vector.memset(tile[:].bitcast(I32), 0)
             return tile
 
-        def stage_scales(name, src, width):
+        def stage_scales(name, src, width, queue):
             tile = keep.tile([P, 2, width // 4], I32, name=name)
             rows = src[0].bitcast(I32).rearrange("(h q r) n -> h r q n", h=2, q=2)
             for h in range(2):
-                nc.sync.dma_start(tile[64 * h:64 * h + 4, :, :], rows[h])
+                queue.dma_start(tile[64 * h:64 * h + 4, :, :], rows[h])
             return tile
 
         def spread_scales(plane, stage):
@@ -68,30 +68,34 @@ def tile_list_boardssum_kernel(tc, xt_words, xt_scales, xo_words, xo_scales, w_w
             for q in range(4):
                 nc.sync.dma_start(plane[32 * q:32 * q + 4, :].bitcast(I32), rows[4 * q:4 * q + 4, :])
 
-        def deal(dst, src):
-            nc.vector.tensor_copy(dst.rearrange("p (t m) -> p t m", t=PACK), src.rearrange("p (m t) -> p t m", t=PACK))
+        def deal(dst, src, t0, t1):
+            nc.vector.tensor_copy(dst.rearrange("p (t m) -> p t m", m=P),
+                                  src.rearrange("p (m t) -> p t m", t=PACK)[:, t0:t1, :])
 
         def fp8_words(ap):
             return ap[0].rearrange("p n t -> p (n t)")
 
+        xt_stage = stage_scales("xt_stage", xt_scales, T, nc.sync)
+        w_stage = stage_scales("w_stage", w_scales, R, nc.scalar)
         o1 = load_list("o1", offs)
-        xt_stage = stage_scales("xt_stage", xt_scales, T)
-        w_stage = stage_scales("w_stage", w_scales, R)
-        xt_w = load_words("xt_w", fp8_words(xt_words), T, U32)
-        w_w = load_words("w_w", w_words[0], 2 * R, U8)
         o3 = load_list("o3", offs3)
+        w_w = load_words("w_w", w_words[0], 2 * R, U8, queue=nc.scalar)
+        xt_w = load_words("xt_w", fp8_words(xt_words), T, U32, tag="xt_then_w")
 
+        xo_s = zero_plane("xo_s", T)
+        w2_planes = sb("w2_planes", 2 * R, U8, "w2s_then_pa4")
+        w2_s, w2_ds = w2_planes[:, 0:R], w2_planes[:, R:2 * R]
+        nc.vector.memset(w2_s.bitcast(I32), 0)
         xt_s = zero_plane("xt_s", T)
         w_s = zero_plane("w_s", R)
-        xo_s = zero_plane("xo_s", T)
-        rest_s = zero_plane("rest_s", R + 2 * N)
-        w2_s, wb_s, wc_s = rest_s[:, 0:R], rest_s[:, R:R + N], rest_s[:, R + N:R + 2 * N]
+        out_s = zero_plane("out_s", 2 * N)
+        wb_s, wc_s = out_s[:, 0:N], out_s[:, N:2 * N]
 
         o2 = load_list("o2", offs2)
         load_plane(xo_s, xo_scales)
-        load_plane(w2_s, w2_scales)
         xo_w = load_words("xo_w", fp8_words(xo_words), T, U32)
         w2_w = load_words("w2_w", w2_words[0], 2 * R, U8)
+        load_plane(w2_s, w2_scales)
         o4 = load_list("o4", offs4)
         load_plane(wb_s, wb_scales)
         load_plane(wc_s, wc_scales)
@@ -107,7 +111,7 @@ def tile_list_boardssum_kernel(tc, xt_words, xt_scales, xo_words, xo_scales, w_w
 
         def new_board():
             board = ring.tile([P, C], F32, name="board", tag="board")
-            nc.vector.memset(board[:], 0.0)
+            nc.gpsimd.memset(board[:], 0.0)
             return board
 
         def bank(tag, name):
@@ -127,50 +131,56 @@ def tile_list_boardssum_kernel(tc, xt_words, xt_scales, xo_words, xo_scales, w_w
         boards_a = [new_board() for t in range(PACK)]
         spread_scales(xt_s, xt_stage)
         spread_scales(w_s, w_stage)
-        xt_g = sb("xt_g", J, U32)
-        xt_gs = sb("xt_gs", J, U8)
-        w_d = sb("w_d", 2 * R, U8)
-        w_ds = sb("w_ds", R, U8)
+        xt_g = sb("xt_g", J, U32, "g_words")
+        xt_gs = sb("xt_gs", J, U8, "g_scales")
+        w_d0 = sb("w_d0", 2 * P, U8)
+        w_ds0 = sb("w_ds0", P, U8)
         nc.vector.tensor_copy(xt_gs[:, 0:HALF], xt_s[:].indirect(o1[:, 0:HALF // 16]))
-        deal(w_ds[:], w_s[:])
-        deal(w_d[:].bitcast(U16), w_w[:].bitcast(U16))
+        deal(w_ds0[:], w_s[:], 0, 1)
+        deal(w_d0[:].bitcast(U16), w_w[:].bitcast(U16), 0, 1)
         nc.vector.tensor_copy(xt_g[:, 0:HALF], xt_w[:].indirect(o1[:, 0:HALF // 16]))
         nc.vector.tensor_copy(xt_gs[:, HALF:J], xt_s[:].indirect(o1[:, HALF // 16:J // 16]))
         nc.vector.tensor_copy(xt_g[:, HALF:J], xt_w[:].indirect(o1[:, HALF // 16:J // 16]))
+        w_rest = sb("w_rest", 9 * P, U8, "xt_then_w")
+        w_d, w_ds = w_rest[:, 0:6 * P], w_rest[:, 6 * P:9 * P]
+        deal(w_d.bitcast(U16), w_w[:].bitcast(U16), 1, PACK)
+        deal(w_ds, w_s[:], 1, PACK)
 
-        a_sb = sb("a_sb", PACK * J, F32)
+        a_lo, a_hi = sb("a_lo", HALF, F32, "a_first"), sb("a_hi", HALF, F32)
         s0 = bank("s0", "a0")
-        first_stage(s0[:, 0:HALF], w_d, w_ds, 0, xt_g, xt_gs, E5M2X4, 0, HALF)
-        nc.scalar.activation(a_sb[:, 0:HALF], s0[:, 0:HALF], COPY)
-        scatter(boards_a[0], o3, a_sb[:, 0:HALF], 0, HALF)
+        first_stage(s0[:, 0:HALF], w_d0, w_ds0, 0, xt_g, xt_gs, E5M2X4, 0, HALF)
+        nc.scalar.activation(a_lo[:], s0[:, 0:HALF], COPY)
+        scatter(boards_a[0], o3, a_lo[:], 0, HALF)
         s1 = bank("s1", "a1")
-        first_stage(s1[:, 0:HALF], w_d, w_ds, 0, xt_g, xt_gs, E5M2X4, HALF, J)
-        first_stage(s1[:, HALF:HALF + J], w_d, w_ds, 1, xt_g, xt_gs, E5M2X4, 0, J)
-        nc.vector.tensor_copy(a_sb[:, HALF:2 * J], s1[:, 0:HALF + J])
+        first_stage(s1[:, 0:HALF], w_d0, w_ds0, 0, xt_g, xt_gs, E5M2X4, HALF, J)
+        nc.vector.tensor_copy(a_hi[:], s1[:, 0:HALF])
+        scatter(boards_a[0], o3, a_hi[:], HALF, J)
+        a_rest = sb("a_rest", 3 * J, F32, "a_first")
         s2 = bank("s2", "a2")
+        first_stage(s2[:, 0:J], w_d, w_ds, 0, xt_g, xt_gs, E5M2X4, 0, J)
+        nc.vector.tensor_copy(a_rest[:, 0:J], s2[:, 0:J])
+        s3 = bank("s3", "a3")
         for t in (2, 3):
-            first_stage(s2[:, (t - 2) * J:(t - 1) * J], w_d, w_ds, t, xt_g, xt_gs, E5M2X4, 0, J)
-        nc.vector.tensor_copy(a_sb[:, 2 * J:4 * J], s2[:])
-        scatter(boards_a[0], o3, a_sb[:, HALF:J], HALF, J)
+            first_stage(s3[:, (t - 2) * J:(t - 1) * J], w_d, w_ds, t - 1, xt_g, xt_gs, E5M2X4, 0, J)
+        nc.vector.tensor_copy(a_rest[:, J:3 * J], s3[:])
         for t in range(1, PACK):
-            scatter(boards_a[t], o3, a_sb[:, t * J:(t + 1) * J], 0, J)
+            scatter(boards_a[t], o3, a_rest[:, (t - 1) * J:t * J], 0, J)
 
-        xo_g = sb("xo_g", J, U32)
-        xo_gs = sb("xo_gs", J, U8)
-        w2_d = sb("w2_d", 2 * R, U8)
-        w2_ds = sb("w2_ds", R, U8)
+        xo_g = sb("xo_g", J, U32, "g_words")
+        xo_gs = sb("xo_gs", J, U8, "g_scales")
+        w2_d = sb("w2_d", 2 * R, U8, "xt_then_w")
         nc.vector.tensor_copy(xo_gs[:], xo_s[:].indirect(o2[:]))
         nc.vector.tensor_copy(xo_g[:], xo_w[:].indirect(o2[:]))
-        deal(w2_ds[:], w2_s)
-        deal(w2_d[:].bitcast(U16), w2_w[:].bitcast(U16))
+        deal(w2_d[:].bitcast(U16), w2_w[:].bitcast(U16), 0, PACK)
+        deal(w2_ds, w2_s, 0, PACK)
         b_sb = sb("b_sb", PACK * J, F32)
-        for pair, tag in enumerate(("s3", "s0")):
+        for pair, tag in enumerate(("s0", "s1")):
             sbank = bank(tag, "b%d" % pair)
             for e in range(2):
                 first_stage(sbank[:, e * J:(e + 1) * J], w2_d, w2_ds, 2 * pair + e, xo_g, xo_gs, E4M3X4, 0, J)
             nc.vector.tensor_copy(b_sb[:, 2 * pair * J:2 * (pair + 1) * J], sbank[:])
 
-        pa4 = sb("pa4", PACK * C, BF16)
+        pa4 = keep.tile([P, PACK * C], BF16, name="pa4", tag="w2s_then_pa4", align_bytes=64)
         for t in range(PACK):
             weave(pa4, boards_a[t], t)
         qa = sb("qa", C, U32)
@@ -205,8 +215,11 @@ def tile_list_boardssum_kernel(tc, xt_words, xt_scales, xo_words, xo_scales, w_w
                                     rhs_scale=qb_s[:, cols], start=False, stop=True)
         for h in range(2):
             cols = slice(CH * h, CH * (h + 1))
-            nc.scalar.activation(p_sb[0][:, cols], acc[0][h][:, 0:CH], COPY)
-            nc.vector.tensor_copy(p_sb[1][:, cols], acc[1][h][:, 0:CH])
+            for i in range(2):
+                if (i, h) == (0, 1):
+                    nc.vector.tensor_copy(p_sb[i][:, cols], acc[i][h][:, 0:CH])
+                else:
+                    nc.scalar.activation(p_sb[i][:, cols], acc[i][h][:, 0:CH], COPY)
 
         picked, scaled = [], []
         for i in range(2):

@@ -30,7 +30,7 @@ def tile_list_boardssum_kernel(tc, xt_words, xt_scales, xo_words, xo_scales, w_w
     with ExitStack() as ctx:
         lists = ctx.enter_context(tc.tile_pool(name="lists", bufs=1))
         keep = ctx.enter_context(tc.tile_pool(name="keep", bufs=1))
-        ring = ctx.enter_context(tc.tile_pool(name="ring", bufs=8))
+        ring = ctx.enter_context(tc.tile_pool(name="ring", bufs=6))
         psum = ctx.enter_context(tc.psum_pool(name="psum", bufs=1))
 
         def sb(name, width, dtype, tag=""):
@@ -111,7 +111,7 @@ def tile_list_boardssum_kernel(tc, xt_words, xt_scales, xo_words, xo_scales, w_w
 
         def new_board():
             board = ring.tile([P, C], F32, name="board", tag="board")
-            nc.gpsimd.memset(board[:], 0.0)
+            nc.vector.memset(board[:], 0.0)
             return board
 
         def bank(tag, name):
@@ -129,6 +129,7 @@ def tile_list_boardssum_kernel(tc, xt_words, xt_scales, xo_words, xo_scales, w_w
             nc.vector.tensor_copy(x4[:, t:PACK * C:PACK], board[:])
 
         boards_a = [new_board() for t in range(PACK)]
+        boards_b = [new_board() for t in range(2)]
         spread_scales(xt_s, xt_stage)
         spread_scales(w_s, w_stage)
         xt_g = sb("xt_g", J, U32, "g_words")
@@ -180,9 +181,14 @@ def tile_list_boardssum_kernel(tc, xt_words, xt_scales, xo_words, xo_scales, w_w
                 first_stage(sbank[:, e * J:(e + 1) * J], w2_d, w2_ds, 2 * pair + e, xo_g, xo_gs, E4M3X4, 0, J)
             nc.vector.tensor_copy(b_sb[:, 2 * pair * J:2 * (pair + 1) * J], sbank[:])
 
-        pa4 = keep.tile([P, PACK * C], BF16, name="pa4", tag="w2s_then_pa4", align_bytes=64)
+        pa_rows = sb("pa_rows", PACK * C, BF16, "w2s_then_pa4")
         for t in range(PACK):
-            weave(pa4, boards_a[t], t)
+            nc.vector.tensor_copy(pa_rows[:, t * C:(t + 1) * C], boards_a[t][:])
+            if t < 2:
+                boards_b.append(new_board())
+        pa4 = sb("pa4", PACK * C, BF16)
+        nc.vector.tensor_copy(pa4[:].rearrange("p (c i t) -> p c t i", i=4, t=PACK),
+                              pa_rows[:].rearrange("p (t c i) -> p c t i", t=PACK, i=4))
         qa = sb("qa", C, U32)
         qa_s = sb("qa_s", C, U8)
         nc.vector.quantize_mx(out=qa[:].bitcast(E4M3X4), scales=qa_s[:], in_=pa4[:])
@@ -197,7 +203,7 @@ def tile_list_boardssum_kernel(tc, xt_words, xt_scales, xo_words, xo_scales, w_w
         qb = sb("qb", C, U32)
         qb_s = sb("qb_s", C, U8)
         for t in range(PACK):
-            board = new_board()
+            board = boards_b[t]
             scatter(board, o4, b_sb[:, t * J:(t + 1) * J], 0, J)
             if t < PACK - 1:
                 weave(pb4, board, t)

@@ -41,9 +41,9 @@ def tile_list_boardssum_kernel(tc, xt_words, xt_scales, xo_words, xo_scales, w_w
             nc.sync.dma_start(tile[:], src)
             return tile
 
-        def load_words(name, src, width, dtype, tag="", queue=nc.sync):
+        def load_words(name, src, width, dtype, tag=""):
             tile = keep.tile([P, width], dtype, name=name, tag=tag, align_bytes=64)
-            queue.dma_start(tile[:].bitcast(I32), src.bitcast(I32))
+            nc.sync.dma_start(tile[:].bitcast(I32), src.bitcast(I32))
             return tile
 
         def zero_plane(name, width):
@@ -51,22 +51,19 @@ def tile_list_boardssum_kernel(tc, xt_words, xt_scales, xo_words, xo_scales, w_w
             nc.vector.memset(tile[:].bitcast(I32), 0)
             return tile
 
-        def stage_scales(name, src, width, queue):
-            tile = keep.tile([P, 2, width // 4], I32, name=name)
-            rows = src[0].bitcast(I32).rearrange("(h q r) n -> h r q n", h=2, q=2)
-            for h in range(2):
-                queue.dma_start(tile[64 * h:64 * h + 4, :, :], rows[h])
+        def stage_scales(name, src, width):
+            tile = keep.tile([P, 4, width // 4], I32, name=name)
+            nc.sync.dma_start(tile[0:4, :, :], src[0].bitcast(I32).rearrange("(q r) n -> r q n", q=4))
             return tile
 
         def spread_scales(plane, stage):
             for q in range(4):
-                first = 64 * (q // 2)
-                nc.vector.tensor_copy(plane[32 * q:32 * q + 4, :].bitcast(I32), stage[first:first + 4, q % 2, :])
+                nc.vector.tensor_copy(plane[32 * q:32 * q + 4, :].bitcast(I32), stage[0:4, q, :])
 
-        def load_plane(plane, src):
+        def load_plane(plane, src, queue=nc.sync, quadrants=range(4)):
             rows = src[0].bitcast(I32)
-            for q in range(4):
-                nc.sync.dma_start(plane[32 * q:32 * q + 4, :].bitcast(I32), rows[4 * q:4 * q + 4, :])
+            for q in quadrants:
+                queue.dma_start(plane[32 * q:32 * q + 4, :].bitcast(I32), rows[4 * q:4 * q + 4, :])
 
         def deal(dst, src, t0, t1):
             nc.vector.tensor_copy(dst.rearrange("p (t m) -> p t m", m=P),
@@ -75,18 +72,19 @@ def tile_list_boardssum_kernel(tc, xt_words, xt_scales, xo_words, xo_scales, w_w
         def fp8_words(ap):
             return ap[0].rearrange("p n t -> p (n t)")
 
-        xt_stage = stage_scales("xt_stage", xt_scales, T, nc.sync)
-        w_stage = stage_scales("w_stage", w_scales, R, nc.scalar)
+        xt_s = zero_plane("xt_s", T)
+        load_plane(xt_s, xt_scales, nc.scalar, range(3))
+        w_stage = stage_scales("w_stage", w_scales, R)
         o1 = load_list("o1", offs)
-        o3 = load_list("o3", offs3)
-        w_w = load_words("w_w", w_words[0], 2 * R, U8, queue=nc.scalar)
+        load_plane(xt_s, xt_scales, nc.sync, range(3, 4))
+        w_w = load_words("w_w", w_words[0], 2 * R, U8)
         xt_w = load_words("xt_w", fp8_words(xt_words), T, U32, tag="xt_then_w")
+        o3 = load_list("o3", offs3)
 
         xo_s = zero_plane("xo_s", T)
         w2_planes = sb("w2_planes", 2 * R, U8, "w2s_then_pa4")
         w2_s, w2_ds = w2_planes[:, 0:R], w2_planes[:, R:2 * R]
         nc.vector.memset(w2_s.bitcast(I32), 0)
-        xt_s = zero_plane("xt_s", T)
         w_s = zero_plane("w_s", R)
         out_s = zero_plane("out_s", 2 * N)
         wb_s, wc_s = out_s[:, 0:N], out_s[:, N:2 * N]
@@ -125,12 +123,12 @@ def tile_list_boardssum_kernel(tc, xt_words, xt_scales, xo_words, xo_scales, w_w
         def scatter(board, o, src, j0, j1):
             nc.scalar.activation(board[:].indirect(o[:, j0 // 16:j1 // 16]), src, COPY)
 
-        def weave(x4, board, t):
-            nc.vector.tensor_copy(x4[:, t:PACK * C:PACK], board[:])
+        def weave(x4, rows, count):
+            nc.vector.tensor_copy(x4[:].rearrange("p (c i t) -> p c t i", i=4, t=PACK)[:, :, 0:count, :],
+                                  rows[:].rearrange("p (t c i) -> p c t i", t=count, i=4))
 
         boards_a = [new_board() for t in range(PACK)]
         boards_b = [new_board() for t in range(2)]
-        spread_scales(xt_s, xt_stage)
         spread_scales(w_s, w_stage)
         xt_g = sb("xt_g", J, U32, "g_words")
         xt_gs = sb("xt_gs", J, U8, "g_scales")
@@ -187,8 +185,7 @@ def tile_list_boardssum_kernel(tc, xt_words, xt_scales, xo_words, xo_scales, w_w
             if t < 2:
                 boards_b.append(new_board())
         pa4 = sb("pa4", PACK * C, BF16)
-        nc.vector.tensor_copy(pa4[:].rearrange("p (c i t) -> p c t i", i=4, t=PACK),
-                              pa_rows[:].rearrange("p (t c i) -> p c t i", t=PACK, i=4))
+        weave(pa4, pa_rows, PACK)
         qa = sb("qa", C, U32)
         qa_s = sb("qa_s", C, U8)
         nc.vector.quantize_mx(out=qa[:].bitcast(E4M3X4), scales=qa_s[:], in_=pa4[:])
@@ -199,15 +196,17 @@ def tile_list_boardssum_kernel(tc, xt_words, xt_scales, xo_words, xo_scales, w_w
                                     lhsT_scale=wb_s[:, P * i:P * (i + 1)], rhs=qa[:, CH * h:CH * (h + 1)].bitcast(E4M3X4),
                                     rhs_scale=qa_s[:, CH * h:CH * (h + 1)], start=True, stop=False)
 
+        last = PACK - 1
+        pb_rows = sb("pb_rows", last * C, BF16)
         pb4 = sb("pb4", PACK * C, BF16)
         qb = sb("qb", C, U32)
         qb_s = sb("qb_s", C, U8)
         for t in range(PACK):
             board = boards_b[t]
             scatter(board, o4, b_sb[:, t * J:(t + 1) * J], 0, J)
-            if t < PACK - 1:
-                weave(pb4, board, t)
-        last = PACK - 1
+            if t < last:
+                nc.vector.tensor_copy(pb_rows[:, t * C:(t + 1) * C], board[:])
+        weave(pb4, pb_rows, last)
         for h in range(2):
             nc.vector.tensor_copy(pb4[:, PACK * CH * h + last:PACK * CH * (h + 1):PACK], board[:, CH * h:CH * (h + 1)])
         p_sb = [sb("p_sb%d" % i, C, F32) for i in range(2)]

from contextlib import ExitStack

import concourse.mybir as mybir

K, T, J, R, C, N, U = 512, 1024, 256, 512, 512, 256, 256
FLOPS = 2 * (2 * K * R * J + 2 * R * N * C)

F32 = mybir.dt.float32
BF16 = mybir.dt.bfloat16
I32 = mybir.dt.int32
U32 = mybir.dt.uint32
U16 = mybir.dt.uint16
U8 = mybir.dt.uint8
E4M3X4 = mybir.dt.float8_e4m3fn_x4
E5M2X4 = mybir.dt.float8_e5m2_x4
E2M1X4 = mybir.dt.float4_e2m1fn_x4
COPY = mybir.ActivationFunctionType.Copy
MAX = mybir.AluOpType.max

P = 128
PACK = 4
HALF = J // 2
CH = C // 2


def tile_list_boardssum_kernel(tc, xt_words, xt_scales, xo_words, xo_scales, w_words, w_scales,
                                     w2_words, w2_scales, wb_words, wb_scales, wc_words, wc_scales,
                                     so, offs, offs2, offs3, offs4, offs5, offs6, out):
    nc = tc.nc
    with ExitStack() as ctx:
        lists = ctx.enter_context(tc.tile_pool(name="lists", bufs=1))
        keep = ctx.enter_context(tc.tile_pool(name="keep", bufs=1))
        ring = ctx.enter_context(tc.tile_pool(name="ring", bufs=6))
        psum = ctx.enter_context(tc.psum_pool(name="psum", bufs=1))

        def sb(name, width, dtype, tag=""):
            return keep.tile([P, width], dtype, name=name, tag=tag, align_bytes=64)

        def load_list(name, src):
            tile = lists.tile([P, J // 16], U16, name=name)
            nc.sync.dma_start(tile[:], src)
            return tile

        def load_words(name, src, width, dtype, tag=""):
            tile = keep.tile([P, width], dtype, name=name, tag=tag, align_bytes=64)
            nc.sync.dma_start(tile[:].bitcast(I32), src.bitcast(I32))
            return tile

        def zero_plane(name, width):
            tile = sb(name, width, U8)
            nc.vector.memset(tile[:].bitcast(I32), 0)
            return tile

        def stage_scales(name, src, width):
            tile = keep.tile([P, 4, width // 4], I32, name=name)
            nc.sync.dma_start(tile[0:4, :, :], src[0].bitcast(I32).rearrange("(q r) n -> r q n", q=4))
            return tile

        def spread_scales(plane, stage):
            for q in range(4):
                nc.vector.tensor_copy(plane[32 * q:32 * q + 4, :].bitcast(I32), stage[0:4, q, :])

        def load_plane(plane, src, queue=nc.sync, quadrants=range(4)):
            rows = src[0].bitcast(I32)
            for q in quadrants:
                queue.dma_start(plane[32 * q:32 * q + 4, :].bitcast(I32), rows[4 * q:4 * q + 4, :])

        def deal(dst, src, t0, t1):
            nc.vector.tensor_copy(dst.rearrange("p (t m) -> p t m", m=P),
                                  src.rearrange("p (m t) -> p t m", t=PACK)[:, t0:t1, :])

        def fp8_words(ap):
            return ap[0].rearrange("p n t -> p (n t)")

        xt_s = zero_plane("xt_s", T)
        load_plane(xt_s, xt_scales, nc.scalar, range(3))
        w_stage = stage_scales("w_stage", w_scales, R)
        o1 = load_list("o1", offs)
        load_plane(xt_s, xt_scales, nc.sync, range(3, 4))
        w_w = load_words("w_w", w_words[0], 2 * R, U8)
        xt_w = load_words("xt_w", fp8_words(xt_words), T, U32, tag="xt_then_w")
        o3 = load_list("o3", offs3)

        xo_s = zero_plane("xo_s", T)
        w2_planes = sb("w2_planes", 2 * R, U8, "w2s_then_pa4")
        w2_s, w2_ds = w2_planes[:, 0:R], w2_planes[:, R:2 * R]
        nc.vector.memset(w2_s.bitcast(I32), 0)
        w_s = zero_plane("w_s", R)
        out_s = zero_plane("out_s", 2 * N)
        wb_s, wc_s = out_s[:, 0:N], out_s[:, N:2 * N]

        o2 = load_list("o2", offs2)
        load_plane(xo_s, xo_scales)
        xo_w = load_words("xo_w", fp8_words(xo_words), T, U32)
        w2_w = load_words("w2_w", w2_words[0], 2 * R, U8)
        load_plane(w2_s, w2_scales)
        o4 = load_list("o4", offs4)
        load_plane(wb_s, wb_scales)
        load_plane(wc_s, wc_scales)
        wb_w = load_words("wb_w", wb_words[0], 2 * N, U8)
        wc_w = load_words("wc_w", fp8_words(wc_words), N, U32)
        o5 = load_list("o5", offs5)
        o6 = load_list("o6", offs6)
        so_t = []
        for i in range(2):
            s = keep.tile([P, 1], F32, name="so%d" % i)
            nc.sync.dma_start(s[:], so[P * i:P * (i + 1), :])
            so_t.append(s)

        def new_board():
            board = ring.tile([P, C], F32, name="board", tag="board")
            nc.vector.memset(board[:], 0.0)
            return board

        def bank(tag, name):
            return psum.tile([P, 512], F32, name=name, tag=tag)

        def first_stage(dst, wd, sd, t, xg, sg, fmt, j0, j1):
            nc.tensor.matmul_mx(out=dst, lhsT=wd[:, 2 * P * t:2 * P * (t + 1)].bitcast(E2M1X4),
                                lhsT_scale=sd[:, P * t:P * (t + 1)], rhs=xg[:, j0:j1].bitcast(fmt),
                                rhs_scale=sg[:, j0:j1], start=True, stop=True)

        def scatter(board, o, src, j0, j1):
            nc.scalar.activation(board[:].indirect(o[:, j0 // 16:j1 // 16]), src, COPY)

        def weave(x4, rows, count):
            nc.vector.tensor_copy(x4[:].rearrange("p (c i t) -> p c t i", i=4, t=PACK)[:, :, 0:count, :],
                                  rows[:].rearrange("p (t c i) -> p c t i", t=count, i=4))

        boards_a = [new_board() for t in range(PACK)]
        boards_b = [new_board() for t in range(2)]
        spread_scales(w_s, w_stage)
        xt_g = sb("xt_g", J, U32, "g_words")
        xt_gs = sb("xt_gs", J, U8, "g_scales")
        w_d0 = sb("w_d0", 2 * P, U8)
        w_ds0 = sb("w_ds0", P, U8)
        nc.vector.tensor_copy(xt_gs[:, 0:HALF], xt_s[:].indirect(o1[:, 0:HALF // 16]))
        deal(w_ds0[:], w_s[:], 0, 1)
        deal(w_d0[:].bitcast(U16), w_w[:].bitcast(U16), 0, 1)
        nc.vector.tensor_copy(xt_g[:, 0:HALF], xt_w[:].indirect(o1[:, 0:HALF // 16]))
        nc.vector.tensor_copy(xt_gs[:, HALF:J], xt_s[:].indirect(o1[:, HALF // 16:J // 16]))
        nc.vector.tensor_copy(xt_g[:, HALF:J], xt_w[:].indirect(o1[:, HALF // 16:J // 16]))
        w_rest = sb("w_rest", 9 * P, U8, "xt_then_w")
        w_d, w_ds = w_rest[:, 0:6 * P], w_rest[:, 6 * P:9 * P]
        deal(w_d.bitcast(U16), w_w[:].bitcast(U16), 1, PACK)
        deal(w_ds, w_s[:], 1, PACK)

        a_lo, a_hi = sb("a_lo", HALF, F32, "a_first"), sb("a_hi", HALF, F32)
        s0 = bank("s0", "a0")
        first_stage(s0[:, 0:HALF], w_d0, w_ds0, 0, xt_g, xt_gs, E5M2X4, 0, HALF)
        nc.scalar.activation(a_lo[:], s0[:, 0:HALF], COPY)
        scatter(boards_a[0], o3, a_lo[:], 0, HALF)
        s1 = bank("s1", "a1")
        first_stage(s1[:, 0:HALF], w_d0, w_ds0, 0, xt_g, xt_gs, E5M2X4, HALF, J)
        nc.vector.tensor_copy(a_hi[:], s1[:, 0:HALF])
        scatter(boards_a[0], o3, a_hi[:], HALF, J)
        a_rest = sb("a_rest", 3 * J, F32, "a_first")
        s2 = bank("s2", "a2")
        first_stage(s2[:, 0:J], w_d, w_ds, 0, xt_g, xt_gs, E5M2X4, 0, J)
        nc.vector.tensor_copy(a_rest[:, 0:J], s2[:, 0:J])
        s3 = bank("s3", "a3")
        for t in (2, 3):
            first_stage(s3[:, (t - 2) * J:(t - 1) * J], w_d, w_ds, t - 1, xt_g, xt_gs, E5M2X4, 0, J)
        nc.vector.tensor_copy(a_rest[:, J:3 * J], s3[:])
        for t in range(1, PACK):
            scatter(boards_a[t], o3, a_rest[:, (t - 1) * J:t * J], 0, J)

        xo_g = sb("xo_g", J, U32, "g_words")
        xo_gs = sb("xo_gs", J, U8, "g_scales")
        w2_d = sb("w2_d", 2 * R, U8, "xt_then_w")
        nc.vector.tensor_copy(xo_gs[:], xo_s[:].indirect(o2[:]))
        nc.vector.tensor_copy(xo_g[:], xo_w[:].indirect(o2[:]))
        deal(w2_d[:].bitcast(U16), w2_w[:].bitcast(U16), 0, PACK)
        deal(w2_ds, w2_s, 0, PACK)
        b_sb = sb("b_sb", PACK * J, F32)
        for pair, tag in enumerate(("s0", "s1")):
            sbank = bank(tag, "b%d" % pair)
            for e in range(2):
                first_stage(sbank[:, e * J:(e + 1) * J], w2_d, w2_ds, 2 * pair + e, xo_g, xo_gs, E4M3X4, 0, J)
            nc.vector.tensor_copy(b_sb[:, 2 * pair * J:2 * (pair + 1) * J], sbank[:])

        pa_rows = sb("pa_rows", PACK * C, BF16, "w2s_then_pa4")
        for t in range(PACK):
            nc.vector.tensor_copy(pa_rows[:, t * C:(t + 1) * C], boards_a[t][:])
            if t < 2:
                boards_b.append(new_board())
        pa4 = sb("pa4", PACK * C, BF16)
        weave(pa4, pa_rows, PACK)
        qa = sb("qa", C, U32)
        qa_s = sb("qa_s", C, U8)
        nc.vector.quantize_mx(out=qa[:].bitcast(E4M3X4), scales=qa_s[:], in_=pa4[:])
        acc = [[bank("p%d%d" % (i, h), "p%d%d" % (i, h)) for h in range(2)] for i in range(2)]
        for i in range(2):
            for h in range(2):
                nc.tensor.matmul_mx(out=acc[i][h][:, 0:CH], lhsT=wb_w[:, 2 * P * i:2 * P * (i + 1)].bitcast(E2M1X4),
                                    lhsT_scale=wb_s[:, P * i:P * (i + 1)], rhs=qa[:, CH * h:CH * (h + 1)].bitcast(E4M3X4),
                                    rhs_scale=qa_s[:, CH * h:CH * (h + 1)], start=True, stop=False)

        last = PACK - 1
        pb_rows = sb("pb_rows", last * C, BF16)
        pb4 = sb("pb4", PACK * C, BF16)
        qb = sb("qb", C, U32)
        qb_s = sb("qb_s", C, U8)
        for t in range(PACK):
            board = boards_b[t]
            scatter(board, o4, b_sb[:, t * J:(t + 1) * J], 0, J)
            if t < last:
                nc.vector.tensor_copy(pb_rows[:, t * C:(t + 1) * C], board[:])
        weave(pb4, pb_rows, last)
        for h in range(2):
            nc.vector.tensor_copy(pb4[:, PACK * CH * h + last:PACK * CH * (h + 1):PACK], board[:, CH * h:CH * (h + 1)])
        p_sb = [sb("p_sb%d" % i, C, F32) for i in range(2)]
        for h in range(2):
            cols = slice(CH * h, CH * (h + 1))
            nc.vector.quantize_mx(out=qb[:, cols].bitcast(E4M3X4), scales=qb_s[:, cols],
                                  in_=pb4[:, PACK * CH * h:PACK * CH * (h + 1)])
            for i in range(2):
                nc.tensor.matmul_mx(out=acc[i][h][:, 0:CH], lhsT=wc_w[:, P * i:P * (i + 1)].bitcast(E4M3X4),
                                    lhsT_scale=wc_s[:, P * i:P * (i + 1)], rhs=qb[:, cols].bitcast(E4M3X4),
                                    rhs_scale=qb_s[:, cols], start=False, stop=True)
        for h in range(2):
            cols = slice(CH * h, CH * (h + 1))
            for i in range(2):
                if (i, h) == (0, 1):
                    nc.vector.tensor_copy(p_sb[i][:, cols], acc[i][h][:, 0:CH])
                else:
                    nc.scalar.activation(p_sb[i][:, cols], acc[i][h][:, 0:CH], COPY)

        picked, scaled = [], []
        for i in range(2):
            sc = sb("scaled%d" % i, U, F32)
            nc.scalar.activation(sc[:], p_sb[i][:].indirect(o5[:]), COPY, scale=so_t[i][:])
            pk = sb("picked%d" % i, U, F32)
            nc.vector.tensor_copy(pk[:], p_sb[i][:].indirect(o6[:]))
            scaled.append(sc)
            picked.append(pk)
        for i in range(2):
            y = sb("y%d" % i, U, F32)
            nc.vector.tensor_tensor(y[:], scaled[i][:], picked[i][:], MAX)
            nc.sync.dma_start(out[P * i:P * (i + 1), :], y[:])
